import numpy as np
import ml_dtypes


def mxq(x, axis, fmt="e4m3"):
    dtype, down = {"e4m3": (ml_dtypes.float8_e4m3fn, 7), "e5m2": (ml_dtypes.float8_e5m2, 14)}[fmt]
    v = np.moveaxis(np.asarray(x, np.float32).astype(ml_dtypes.bfloat16).astype(np.float64), axis, -1)
    blocks = v.reshape(v.shape[:-1] + (-1, 32))
    amax = np.abs(blocks).max(-1, keepdims=True)
    byte = np.maximum(np.where(amax > 0, np.frexp(amax)[1] - 1 + 127, 0) - down, 1)
    scale = np.exp2(byte - 127.0)
    codes = (blocks / scale).astype(np.float32).astype(dtype).astype(np.float64)
    return np.moveaxis((codes * scale).reshape(v.shape), -1, axis)


WIDE = False


def mx_kscale(k):
    if not WIDE:
        return np.ones(k)
    levels = np.array([10, -10, 5, -5, 0])
    if k % 512:
        return np.exp2(np.random.permutation(np.resize(levels, k // 32))).repeat(32)
    a = np.empty((k // 512, 16))
    for p in range(k // 512):
        a[p, :8] = np.random.permutation(np.resize(levels, 8))
        for g in range(8):
            far = levels[np.abs(levels - a[p, g]) >= 10]
            a[p, g + 8] = far[np.random.randint(len(far))]
    return np.exp2(a.ravel()).repeat(32)


def f64(x):
    return np.asarray(x).astype(np.float64)


def striped(idx):
    return np.tile(idx.reshape(-1, 16).T, (8, 1)).astype(np.uint16)


def unstriped(offs):
    return offs[:16].T.reshape(-1).astype(np.int64)


E2M1 = np.array([0.0, 0.5, 1.0, 1.5, 2.0, 3.0, 4.0, 6.0, -0.0, -0.5, -1.0, -1.5, -2.0, -3.0, -4.0, -6.0])


def pack_weight(w, fmt):
    k, n = w.shape
    w = f64(np.asarray(w, np.float32).astype(ml_dtypes.bfloat16)).reshape(k // 32, 32, n)
    amax = np.abs(w).max(1)
    if fmt == "e4m3":
        byte = np.frexp(amax)[1] - 1 + 127 - 7
    else:
        mant, ex = np.frexp(amax / 6.0)
        byte = np.where(mant > 0.5, ex, ex - 1) + 127
    byte = np.clip(np.where(amax > 0, byte, 1), 1, 254)
    scaled = (w * np.exp2(127.0 - byte)[:, None, :]).reshape(k, n).astype(np.float32)
    by_word = np.ascontiguousarray(scaled.reshape(k // 512, 128, 4, n).transpose(0, 1, 3, 2))
    if fmt == "e4m3":
        words = by_word.astype(ml_dtypes.float8_e4m3fn).view(np.uint8)
    else:
        c = by_word.astype(ml_dtypes.float4_e2m1fn).view(np.uint8) & 0xF
        words = (c[..., 0::2] | (c[..., 1::2] << 4)).reshape(k // 512, 128, 2 * n)
    return np.ascontiguousarray(words), np.ascontiguousarray(byte.astype(np.uint8).reshape(k // 512, 16, n))


def unpack_weight(words, scales, fmt):
    g, _, n = scales.shape
    words = np.ascontiguousarray(words).reshape(g, 128, n, -1)
    if fmt == "e4m3":
        vals = words.view(ml_dtypes.float8_e4m3fn).astype(np.float64)
    else:
        nib = np.empty((g, 128, n, 4), np.uint8)
        nib[..., 0::2] = words & 0xF
        nib[..., 1::2] = words >> 4
        vals = E2M1[nib]
    vals = vals * np.repeat(np.exp2(scales.astype(np.float64) - 127.0), 8, axis=1)[..., None]
    return vals.transpose(0, 1, 3, 2).reshape(g * 512, n)


def gelu(v):
    return 0.5 * v * (1.0 + np.tanh(np.sqrt(2.0 / np.pi) * (v + 0.044715 * v**3)))


def bf(x):
    return np.asarray(x, np.float32).astype(ml_dtypes.bfloat16)


def planes(Y):
    n, m = Y.shape
    b = f64(bf(Y)).reshape(n // 32, 32, m)
    amax = np.abs(b).max(1)
    byte = np.clip(np.where(amax > 0, np.frexp(amax)[1] - 1 + 127 - 7, 1), 1, 254)
    codes = (b * np.exp2(127.0 - byte)[:, None, :]).reshape(n, m).astype(np.float32).astype(ml_dtypes.float8_e4m3fn).view(np.uint8)
    words = codes.reshape(n // 512, 128, 4, m).transpose(0, 1, 3, 2)
    return np.ascontiguousarray(words), np.ascontiguousarray(byte.astype(np.uint8).reshape(n // 512, 16, m))


K, T, S, H, T2, P, N = 1024, 4096, 1024, 512, 2048, 512, 384

def setup_inputs():
    n = np.random.standard_normal
    s = mx_kscale(K)[:, None]
    u = mx_kscale(H)[:, None]
    d = {}
    d["tab_words"], d["tab_scales"] = pack_weight(n((K, T)) * s, "e4m3")
    d["offs"] = striped(np.random.permutation(T)[:S])
    d["offs2"] = striped(np.random.permutation(T2)[:S])
    d["offs3"] = striped(np.random.permutation(T2)[:P])
    d["w1"] = (n((K, H)) / K ** 0.5 / s).astype(np.float32)
    d["w2_words"], d["w2_scales"] = pack_weight(0.4 * n((K, H)) / K ** 0.5 / s, "e4m3")
    d["ph"] = np.random.uniform(-0.7, 0.7, H).astype(np.float32)
    d["gain"] = (np.exp(0.3 * n(H)) * u[:, 0]).astype(np.float32)
    d["wgs"] = np.exp(0.3 * n((128, S))).astype(np.float32)
    d["page0"] = (n((H, T2)) * u).astype(np.float32)
    d["cell"] = np.exp(0.3 * n(H)).astype(np.float32)
    d["w4_words"], d["w4_scales"] = pack_weight(n((H, N)) / H ** 0.5 / u, "e2m1")
    d["moon"] = (n((N, P)) + 0.5).astype(np.float32)
    return d

def reference(tab_words, tab_scales, offs, offs2, offs3, w1, w2_words, w2_scales, ph, gain, wgs, page0, cell, w4_words, w4_scales, moon):
    v = unpack_weight(tab_words, tab_scales, "e4m3")[:, unstriped(offs)]
    a = mxq(f64(w1), 0, "e4m3").T @ v
    b = unpack_weight(w2_words, w2_scales, "e4m3").T @ v
    h = f64(gain)[:, None] * (a * np.cos(b + f64(ph)[:, None]))
    page = f64(page0).copy()
    page[:, unstriped(offs2)] = np.tile(f64(wgs), (H // 128, 1)) * h
    x = page[:, unstriped(offs3)] * f64(cell)[:, None]
    y = unpack_weight(w4_words, w4_scales, "e2m1").T @ mxq(x, 0, "e4m3")
    y = np.minimum(y, f64(moon))
    words, scales = planes(page)
    return y, page, words, scales

@@ -1,0 +1,245 @@
+import math
+from contextlib import ExitStack
+
+import concourse.mybir as mybir
+
+K, T, S, H, T2, NX, N = 1024, 4096, 1024, 512, 2048, 512, 384
+FLOPS = 2 * K * H * S * 2 + 2 * H * N * NX
+
+F32 = mybir.dt.float32
+BF16 = mybir.dt.bfloat16
+I32 = mybir.dt.int32
+U32 = mybir.dt.uint32
+U16 = mybir.dt.uint16
+U8 = mybir.dt.uint8
+FP8X4 = mybir.dt.float8_e4m3fn_x4
+FP4X4 = mybir.dt.float4_e2m1fn_x4
+ACT = mybir.ActivationFunctionType
+ALU = mybir.AluOpType
+
+P = 128
+PACK = 4
+PASSES = K // (P * PACK)
+BANK = 512
+QUADS = 4
+QUAD_ORDER = (0, 2, 1, 3)
+CHUNK = 512
+
+
+def tile_list_firefly_phase_board_kernel(
+    tc, tab_words, tab_scales, offs, offs2, offs3, w1, w2_words, w2_scales, ph, gain, wgs, page0, cell,
+    w4_words, w4_scales, moon, out_0, out_1, out_2, out_3,
+):
+    nc = tc.nc
+    with ExitStack() as ctx:
+        keep = ctx.enter_context(tc.tile_pool(name="keep", bufs=1))
+        ring = ctx.enter_context(tc.tile_pool(name="ring", bufs=2))
+        psum_b = ctx.enter_context(tc.psum_pool(name="psum_b", bufs=3))
+        psum_a = ctx.enter_context(tc.psum_pool(name="psum_a", bufs=4))
+
+        idx = keep.tile([P, S // 16], U16, name="idx")
+        idx2 = keep.tile([P, S // 16], U16, name="idx2")
+        idx3 = keep.tile([P, NX // 16], U16, name="idx3")
+        tab_w = [keep.tile([P, T], I32, name=f"tab_w{a}", align_bytes=64) for a in range(PASSES)]
+        tab_s = keep.tile([P, T], U8, name="tab_s", align_bytes=64)
+        w2_w = keep.tile([P, PASSES, H], I32, name="w2_w", align_bytes=64)
+        w2_s = keep.tile([P, H], U8, name="w2_s", align_bytes=64)
+        w4_w = keep.tile([P, 2 * N], U8, name="w4_w", align_bytes=64)
+        w4_s = keep.tile([P, N], U8, name="w4_s", align_bytes=64)
+        ph_t = keep.tile([P, PACK], F32, name="ph_t")
+        gain_t = keep.tile([P, PACK], F32, name="gain_t")
+        cell_t = keep.tile([P, PACK], F32, name="cell_t")
+        w1_parts = [(0, 0, H), (1, 0, H // 2), (1, H // 2, H)]
+        w1_raw = [keep.tile([P, PACK, c1 - c0], F32, name=f"w1_raw{i}") for i, (a, c0, c1) in enumerate(w1_parts)]
+        wgs_first = keep.tile([P, S], F32, name="wgs_first")
+        wgs_rest = keep.tile([P, PACK - 1, S], F32, name="wgs_rest")
+        page = [keep.tile([P, T2], F32, name=f"page{t}") for t in range(PACK)]
+        moon_t = keep.tile([P, N // P, NX], F32, name="moon_t")
+
+        for plane in (tab_s, w2_s, w4_s):
+            nc.vector.memset(plane[:].bitcast(I32), 0)
+        for q in range(QUADS):
+            nc.gpsimd.dma_start(
+                out=tab_s[32 * q : 32 * q + 4 * PASSES, :].bitcast(I32),
+                in_=tab_scales[:, 4 * q : 4 * q + 4, :].bitcast(I32),
+            )
+
+        def load_table(a):
+            nc.sync.dma_start(out=tab_w[a][:], in_=tab_words[a].rearrange("p t i -> p (t i)").bitcast(I32))
+
+        def load_page(t):
+            nc.sync.dma_start(out=page[t][:], in_=page0.rearrange("(p t) m -> t p m", t=PACK)[t])
+
+        wgs_dealt = wgs.rearrange("(p t) j -> p t j", t=PACK)
+        load_table(0)
+        nc.sync.dma_start(idx[:], offs)
+        nc.sync.dma_start(out=w2_w[:], in_=w2_words.rearrange("a p c i -> p a (c i)").bitcast(I32))
+        for q in range(QUADS):
+            nc.sync.dma_start(
+                out=w2_s[32 * q : 32 * q + 4 * PASSES, :].bitcast(I32),
+                in_=w2_scales[:, 4 * q : 4 * q + 4, :].bitcast(I32),
+            )
+        load_table(1)
+        nc.sync.dma_start(out=ph_t[:], in_=ph.rearrange("(p t) -> p t", t=PACK))
+        nc.sync.dma_start(out=gain_t[:], in_=gain.rearrange("(p t) -> p t", t=PACK))
+        nc.sync.dma_start(idx2[:], offs2)
+        for raw, (a, c0, c1) in zip(w1_raw, w1_parts):
+            rows = w1[a * P * PACK : (a + 1) * P * PACK, c0:c1]
+            nc.sync.dma_start(out=raw[:], in_=rows.rearrange("(p j) c -> p j c", j=PACK))
+        for q in QUAD_ORDER:
+            nc.sync.dma_start(out=wgs_first[32 * q : 32 * q + 32, :], in_=wgs_dealt[:, 0, :])
+        load_page(0)
+        nc.sync.dma_start(idx3[:], offs3)
+        nc.sync.dma_start(out=cell_t[:], in_=cell.rearrange("(p t) -> p t", t=PACK))
+        load_page(1)
+        for q in QUAD_ORDER:
+            nc.sync.dma_start(out=wgs_rest[32 * q : 32 * q + 32, :, :], in_=wgs_dealt[:, 1:, :])
+        load_page(2)
+        load_page(3)
+        nc.sync.dma_start(out=w4_w[:].bitcast(I32), in_=w4_words[0].bitcast(I32))
+        for q in range(QUADS):
+            nc.sync.dma_start(
+                out=w4_s[32 * q : 32 * q + 4, :].bitcast(I32),
+                in_=w4_scales[0, 4 * q : 4 * q + 4, :].bitcast(I32),
+            )
+        nc.sync.dma_start(out=moon_t[:], in_=moon.rearrange("(c p) j -> p c j", p=P))
+
+        v_s = keep.tile([P, S], U8, name="v_s", align_bytes=64)
+        nc.vector.tensor_copy(v_s[:], tab_s[:].indirect(idx[:]))
+        v_w = [
+            keep.tile([P, S], U32, name="v_w0", align_bytes=64),
+            keep.tile([P, S], U32, name="v_w1", tag="tab_s", align_bytes=64),
+        ]
+        nc.vector.tensor_copy(v_w[0][:], tab_w[0][:].bitcast(U32).indirect(idx[:]))
+
+        w2_wd = keep.tile([P, PASSES, H], I32, name="w2_wd", align_bytes=64)
+        w2_sd = keep.tile([P, H], U8, name="w2_sd", align_bytes=64)
+        nc.vector.tensor_copy(
+            out=w2_sd[:].rearrange("p (t m) -> p m t", t=PACK), in_=w2_s[:].rearrange("p (m t) -> p m t", t=PACK)
+        )
+        for a in range(PASSES):
+            nc.vector.tensor_copy(
+                out=w2_wd[:, a, :].rearrange("p (t c i) -> p c t i", t=PACK, i=4),
+                in_=w2_w[:, a, :].rearrange("p (c i t) -> p c t i", t=PACK, i=4),
+            )
+
+        for h0 in range(0, S, BANK):
+            nc.vector.tensor_copy(
+                v_w[1][:, h0 : h0 + BANK], tab_w[1][:].bitcast(U32).indirect(idx[:, h0 // 16 : (h0 + BANK) // 16])
+            )
+
+        cosb = [keep.tile([P, S], F32, name=f"cosb{t}") for t in range(PACK)]
+        for t in range(PACK):
+            for h0 in range(0, S, BANK):
+                acc_b = psum_b.tile([P, BANK], F32, name="acc_b")
+                for a in range(PASSES):
+                    nc.tensor.matmul_mx(
+                        out=acc_b[:],
+                        lhsT=w2_wd[:, a, t * P : (t + 1) * P].bitcast(FP8X4),
+                        lhsT_scale=w2_sd[4 * a : P, t * P : (t + 1) * P],
+                        rhs=v_w[a][:, h0 : h0 + BANK].bitcast(FP8X4),
+                        rhs_scale=v_s[4 * a : P, h0 : h0 + BANK],
+                        start=(a == 0),
+                        stop=(a == PASSES - 1),
+                    )
+                angle = ring.tile([P, BANK], F32, name="angle")
+                nc.scalar.activation(angle[:], acc_b[:], ACT.Abs, bias=ph_t[:, t : t + 1])
+                nc.scalar.activation(cosb[t][:, h0 : h0 + BANK], angle[:], ACT.Sin, bias=math.pi / 2, scale=-1.0)
+
+        w1_g = [keep.tile([P, H * PACK], BF16, name=f"w1_g{a}", tag=f"tab_w{1 - a}", align_bytes=64) for a in range(PASSES)]
+        w1_w = [keep.tile([P, H], U32, name=f"w1_w{a}", align_bytes=64) for a in range(PASSES)]
+        w1_s = [keep.tile([P, H], U8, name=f"w1_s{a}", align_bytes=64) for a in range(PASSES)]
+        for raw, (a, c0, c1) in zip(w1_raw, w1_parts):
+            nc.vector.tensor_copy(
+                out=w1_g[a][:].rearrange("p (t m j) -> p m t j", t=PACK, j=PACK)[:, c0 // PACK : c1 // PACK],
+                in_=raw[:].rearrange("p j (m t) -> p m t j", t=PACK),
+            )
+            if c1 == H:
+                nc.vector.quantize_mx(out=w1_w[a][:].bitcast(FP8X4), scales=w1_s[a][:], in_=w1_g[a][:])
+
+        chunks = [slice(c0, c0 + CHUNK) for c0 in range(0, T2, CHUNK)]
+        pairs = [keep.tile([P, 2, CHUNK, 2], BF16, name=f"pairs{c}") for c in range(len(chunks))]
+        x_g = keep.tile([P, NX, PACK], BF16, name="x_g", align_bytes=64)
+        for t in range(PACK):
+            feat = keep.tile([P, S], F32, name=f"feat{t}")
+            for h0 in range(0, S, BANK):
+                acc_a = psum_a.tile([P, BANK], F32, name="acc_a")
+                for a in range(PASSES):
+                    nc.tensor.matmul_mx(
+                        out=acc_a[:],
+                        lhsT=w1_w[a][:, t * P : (t + 1) * P].bitcast(FP8X4),
+                        lhsT_scale=w1_s[a][:, t * P : (t + 1) * P],
+                        rhs=v_w[a][:, h0 : h0 + BANK].bitcast(FP8X4),
+                        rhs_scale=v_s[4 * a : P, h0 : h0 + BANK],
+                        start=(a == 0),
+                        stop=(a == PASSES - 1),
+                    )
+                nc.vector.scalar_tensor_tensor(
+                    out=feat[:, h0 : h0 + BANK], in0=acc_a[:], scalar=gain_t[:, t : t + 1],
+                    in1=cosb[t][:, h0 : h0 + BANK], op0=ALU.mult, op1=ALU.mult,
+                )
+            weights = wgs_first[:] if t == 0 else wgs_rest[:, t - 1, :]
+            nc.vector.tensor_tensor(page[t][:].indirect(idx2[:]), feat[:], weights, ALU.mult)
+            nc.sync.dma_start(out=out_1.rearrange("(p t) m -> t p m", t=PACK)[t], in_=page[t][:])
+            picked = ring.tile([P, NX], F32, name="picked")
+            nc.vector.tensor_copy(picked[:], page[t][:].indirect(idx3[:]))
+            if t < PACK - 1:
+                nc.scalar.activation(x_g[:, :, t], picked[:], ACT.Copy, scale=cell_t[:, t : t + 1])
+                for c, cols in enumerate(chunks):
+                    nc.scalar.copy(pairs[c][:, t // 2, :, t % 2], page[t][:, cols])
+
+        t = PACK - 1
+        plane_w = keep.tile([P, T2], I32, name="plane_w", align_bytes=64)
+        plane_s = keep.tile([P, T2], U8, name="plane_s", align_bytes=64)
+        x_w = keep.tile([P, NX], U32, name="x_w", align_bytes=64)
+        x_s = keep.tile([P, NX], U8, name="x_s", align_bytes=64)
+        out_words = out_2[0].rearrange("p m t -> p (m t)").bitcast(I32)
+
+        grouped = [keep.tile([P, CHUNK * PACK], BF16, name=f"grouped{c}", align_bytes=64) for c in range(len(chunks))]
+
+        def round_last(c):
+            nc.scalar.copy(pairs[c][:, t // 2, :, t % 2], page[t][:, chunks[c]])
+
+        def weave(c, copy, word):
+            copy(
+                grouped[c][:].bitcast(word).rearrange("p (m u) -> p m u", u=2),
+                pairs[c][:].rearrange("p u m e -> p u (m e)").bitcast(word).rearrange("p u m -> p m u"),
+            )
+
+        def quantise_page(c):
+            cols = chunks[c]
+            nc.vector.quantize_mx(out=plane_w[:, cols].bitcast(FP8X4), scales=plane_s[:, cols], in_=grouped[c][:])
+            nc.sync.dma_start(out=out_words[:, cols], in_=plane_w[:, cols])
+
+        round_last(0)
+        round_last(1)
+        nc.scalar.activation(x_g[:, :, t], picked[:], ACT.Copy, scale=cell_t[:, t : t + 1])
+        round_last(2)
+        round_last(3)
+        weave(0, nc.vector.tensor_copy, I32)
+        weave(1, nc.vector.tensor_copy, I32)
+        quantise_page(0)
+        quantise_page(1)
+        nc.vector.quantize_mx(out=x_w[:].bitcast(FP8X4), scales=x_s[:], in_=x_g[:].rearrange("p j t -> p (j t)"))
+        weave(2, nc.vector.tensor_copy, I32)
+        weave(3, nc.scalar.copy, F32)
+        quantise_page(2)
+        quantise_page(3)
+        for q in range(QUADS):
+            nc.scalar.dma_start(
+                out=out_3[0, 4 * q : 4 * q + 4, :].bitcast(I32), in_=plane_s[32 * q : 32 * q + 4, :].bitcast(I32)
+            )
+        for c in range(N // P):
+            acc_y = psum_b.tile([P, BANK], F32, name="acc_b")
+            nc.tensor.matmul_mx(
+                out=acc_y[:],
+                lhsT=w4_w[:, 2 * c * P : 2 * (c + 1) * P].bitcast(FP4X4),
+                lhsT_scale=w4_s[:, c * P : (c + 1) * P],
+                rhs=x_w[:].bitcast(FP8X4),
+                rhs_scale=x_s[:],
+                start=True,
+                stop=True,
+            )
+            score = keep.tile([P, NX], F32, name=f"score{c}")
+            nc.vector.tensor_tensor(score[:], acc_y[:], moon_t[:, c, :], ALU.min)
+            nc.sync.dma_start(out=out_0[c * P : (c + 1) * P, :], in_=score[:])

@@ -24,6 +24,8 @@ BANK = 512
 QUADS = 4
 QUAD_ORDER = (0, 2, 1, 3)
 CHUNK = 512
+PHASE_BANKS = (0, 2, 0, 4)
+FLASH_BANKS = (4, 6, 2, 6)
 
 
 def tile_list_firefly_phase_board_kernel(
@@ -34,14 +36,14 @@ def tile_list_firefly_phase_board_kernel(
     with ExitStack() as ctx:
         keep = ctx.enter_context(tc.tile_pool(name="keep", bufs=1))
         ring = ctx.enter_context(tc.tile_pool(name="ring", bufs=2))
-        psum_b = ctx.enter_context(tc.psum_pool(name="psum_b", bufs=3))
-        psum_a = ctx.enter_context(tc.psum_pool(name="psum_a", bufs=4))
+        psum = ctx.enter_context(tc.psum_pool(name="psum", bufs=1))
 
         idx = keep.tile([P, S // 16], U16, name="idx")
         idx2 = keep.tile([P, S // 16], U16, name="idx2")
         idx3 = keep.tile([P, NX // 16], U16, name="idx3")
         tab_w = [keep.tile([P, T], I32, name=f"tab_w{a}", align_bytes=64) for a in range(PASSES)]
         tab_s = keep.tile([P, T], U8, name="tab_s", align_bytes=64)
+        v_s = keep.tile([P, PASSES * S], U8, name="v_s", align_bytes=64)
         w2_w = keep.tile([P, PASSES, H], I32, name="w2_w", align_bytes=64)
         w2_s = keep.tile([P, H], U8, name="w2_s", align_bytes=64)
         w4_w = keep.tile([P, 2 * N], U8, name="w4_w", align_bytes=64)
@@ -51,18 +53,16 @@ def tile_list_firefly_phase_board_kernel(
         cell_t = keep.tile([P, PACK], F32, name="cell_t")
         w1_parts = [(0, 0, H), (1, 0, H // 2), (1, H // 2, H)]
         w1_raw = [keep.tile([P, PACK, c1 - c0], F32, name=f"w1_raw{i}") for i, (a, c0, c1) in enumerate(w1_parts)]
-        wgs_first = keep.tile([P, S], F32, name="wgs_first")
-        wgs_rest = keep.tile([P, PACK - 1, S], F32, name="wgs_rest")
+        wgs_t = [keep.tile([P, S], F32, name=f"wgs{t}") for t in range(PACK)]
         page = [keep.tile([P, T2], F32, name=f"page{t}") for t in range(PACK)]
         moon_t = keep.tile([P, N // P, NX], F32, name="moon_t")
 
-        for plane in (tab_s, w2_s, w4_s):
+        warm = keep.tile([P, 2], F32, name="warm")
+        nc.vector.memset(warm[:, 0:1], 0.0)
+        nc.scalar.activation(warm[:, 1:2], warm[:, 0:1], ACT.Sin)
+
+        for plane in (tab_s, w2_s, v_s, w4_s):
             nc.vector.memset(plane[:].bitcast(I32), 0)
-        for q in range(QUADS):
-            nc.gpsimd.dma_start(
-                out=tab_s[32 * q : 32 * q + 4 * PASSES, :].bitcast(I32),
-                in_=tab_scales[:, 4 * q : 4 * q + 4, :].bitcast(I32),
-            )
 
         def load_table(a):
             nc.sync.dma_start(out=tab_w[a][:], in_=tab_words[a].rearrange("p t i -> p (t i)").bitcast(I32))
@@ -70,32 +70,42 @@ def tile_list_firefly_phase_board_kernel(
         def load_page(t):
             nc.sync.dma_start(out=page[t][:], in_=page0.rearrange("(p t) m -> t p m", t=PACK)[t])
 
-        wgs_dealt = wgs.rearrange("(p t) j -> p t j", t=PACK)
-        load_table(0)
-        nc.sync.dma_start(idx[:], offs)
+        def load_wgs(t):
+            for q in QUAD_ORDER:
+                nc.sync.dma_start(
+                    out=wgs_t[t][32 * q : 32 * q + 32, :], in_=wgs.rearrange("(p t) j -> p t j", t=PACK)[:, t, :]
+                )
+
         nc.sync.dma_start(out=w2_w[:], in_=w2_words.rearrange("a p c i -> p a (c i)").bitcast(I32))
+        nc.sync.dma_start(idx[:], offs)
+        for a in range(PASSES):
+            nc.sync.dma_start(out=tab_s[4 * a : P : 8, :].bitcast(I32), in_=tab_scales[a].bitcast(I32))
+        nc.sync.dma_start(out=ph_t[:], in_=ph.rearrange("(p t) -> p t", t=PACK))
+        nc.sync.dma_start(out=gain_t[:], in_=gain.rearrange("(p t) -> p t", t=PACK))
+        nc.sync.dma_start(idx2[:], offs2)
+        load_table(0)
         for q in range(QUADS):
             nc.sync.dma_start(
                 out=w2_s[32 * q : 32 * q + 4 * PASSES, :].bitcast(I32),
                 in_=w2_scales[:, 4 * q : 4 * q + 4, :].bitcast(I32),
             )
         load_table(1)
-        nc.sync.dma_start(out=ph_t[:], in_=ph.rearrange("(p t) -> p t", t=PACK))
-        nc.sync.dma_start(out=gain_t[:], in_=gain.rearrange("(p t) -> p t", t=PACK))
-        nc.sync.dma_start(idx2[:], offs2)
+        v_rows = keep.tile([P, S], U8, name="v_rows", align_bytes=64)
+        nc.vector.tensor_copy(v_rows[:], tab_s[:].indirect(idx[:]))
+        for q in range(QUADS):
+            nc.sync.dma_start(
+                out=v_s[32 * q : 32 * q + 4, :].bitcast(I32), in_=v_rows[32 * q : 32 * q + 32 : 4, :].bitcast(I32)
+            )
         for raw, (a, c0, c1) in zip(w1_raw, w1_parts):
             rows = w1[a * P * PACK : (a + 1) * P * PACK, c0:c1]
             nc.sync.dma_start(out=raw[:], in_=rows.rearrange("(p j) c -> p j c", j=PACK))
-        for q in QUAD_ORDER:
-            nc.sync.dma_start(out=wgs_first[32 * q : 32 * q + 32, :], in_=wgs_dealt[:, 0, :])
+        load_wgs(0)
         load_page(0)
         nc.sync.dma_start(idx3[:], offs3)
         nc.sync.dma_start(out=cell_t[:], in_=cell.rearrange("(p t) -> p t", t=PACK))
-        load_page(1)
-        for q in QUAD_ORDER:
-            nc.sync.dma_start(out=wgs_rest[32 * q : 32 * q + 32, :, :], in_=wgs_dealt[:, 1:, :])
-        load_page(2)
-        load_page(3)
+        for t in range(1, PACK):
+            load_wgs(t)
+            load_page(t)
         nc.sync.dma_start(out=w4_w[:].bitcast(I32), in_=w4_words[0].bitcast(I32))
         for q in range(QUADS):
             nc.sync.dma_start(
@@ -104,12 +114,7 @@ def tile_list_firefly_phase_board_kernel(
             )
         nc.sync.dma_start(out=moon_t[:], in_=moon.rearrange("(c p) j -> p c j", p=P))
 
-        v_s = keep.tile([P, S], U8, name="v_s", align_bytes=64)
-        nc.vector.tensor_copy(v_s[:], tab_s[:].indirect(idx[:]))
-        v_w = [
-            keep.tile([P, S], U32, name="v_w0", align_bytes=64),
-            keep.tile([P, S], U32, name="v_w1", tag="tab_s", align_bytes=64),
-        ]
+        v_w = [keep.tile([P, S], U32, name=f"v_w{a}", align_bytes=64) for a in range(PASSES)]
         nc.vector.tensor_copy(v_w[0][:], tab_w[0][:].bitcast(U32).indirect(idx[:]))
 
         w2_wd = keep.tile([P, PASSES, H], I32, name="w2_wd", align_bytes=64)
@@ -128,25 +133,7 @@ def tile_list_firefly_phase_board_kernel(
                 v_w[1][:, h0 : h0 + BANK], tab_w[1][:].bitcast(U32).indirect(idx[:, h0 // 16 : (h0 + BANK) // 16])
             )
 
-        cosb = [keep.tile([P, S], F32, name=f"cosb{t}") for t in range(PACK)]
-        for t in range(PACK):
-            for h0 in range(0, S, BANK):
-                acc_b = psum_b.tile([P, BANK], F32, name="acc_b")
-                for a in range(PASSES):
-                    nc.tensor.matmul_mx(
-                        out=acc_b[:],
-                        lhsT=w2_wd[:, a, t * P : (t + 1) * P].bitcast(FP8X4),
-                        lhsT_scale=w2_sd[4 * a : P, t * P : (t + 1) * P],
-                        rhs=v_w[a][:, h0 : h0 + BANK].bitcast(FP8X4),
-                        rhs_scale=v_s[4 * a : P, h0 : h0 + BANK],
-                        start=(a == 0),
-                        stop=(a == PASSES - 1),
-                    )
-                angle = ring.tile([P, BANK], F32, name="angle")
-                nc.scalar.activation(angle[:], acc_b[:], ACT.Abs, bias=ph_t[:, t : t + 1])
-                nc.scalar.activation(cosb[t][:, h0 : h0 + BANK], angle[:], ACT.Sin, bias=math.pi / 2, scale=-1.0)
-
-        w1_g = [keep.tile([P, H * PACK], BF16, name=f"w1_g{a}", tag=f"tab_w{1 - a}", align_bytes=64) for a in range(PASSES)]
+        w1_g = [keep.tile([P, H * PACK], BF16, name=f"w1_g{a}", align_bytes=64) for a in range(PASSES)]
         w1_w = [keep.tile([P, H], U32, name=f"w1_w{a}", align_bytes=64) for a in range(PASSES)]
         w1_s = [keep.tile([P, H], U8, name=f"w1_s{a}", align_bytes=64) for a in range(PASSES)]
         for raw, (a, c0, c1) in zip(w1_raw, w1_parts):
@@ -155,33 +142,68 @@ def tile_list_firefly_phase_board_kernel(
                 in_=raw[:].rearrange("p j (m t) -> p m t j", t=PACK),
             )
             if c1 == H:
-                nc.vector.quantize_mx(out=w1_w[a][:].bitcast(FP8X4), scales=w1_s[a][:], in_=w1_g[a][:])
+                for n0, n1 in ((0, H),) if a == 0 else ((0, P), (P, 2 * P), (2 * P, H)):
+                    nc.vector.quantize_mx(
+                        out=w1_w[a][:, n0:n1].bitcast(FP8X4),
+                        scales=w1_s[a][:, n0:n1],
+                        in_=w1_g[a][:, PACK * n0 : PACK * n1],
+                    )
+
+        def first_stage(acc, words, scales, first_row, t, h0, passes):
+            for a in passes:
+                nc.tensor.matmul_mx(
+                    out=acc[:],
+                    lhsT=words[a][:, t * P : (t + 1) * P].bitcast(FP8X4),
+                    lhsT_scale=scales[a][first_row * a : P, t * P : (t + 1) * P],
+                    rhs=v_w[a][:, h0 : h0 + BANK].bitcast(FP8X4),
+                    rhs_scale=v_s[:, a * S + h0 : a * S + h0 + BANK],
+                    start=(a == 0),
+                    stop=(a == PASSES - 1),
+                )
+
+        cosb = [keep.tile([P, S], F32, name=f"cosb{t}") for t in range(PACK)]
+
+        def phase(t):
+            for h0 in range(0, S, BANK):
+                acc_b = psum.tile([P, BANK], F32, name=f"bank{PHASE_BANKS[t] + h0 // BANK}")
+                first_stage(acc_b, [w2_wd[:, a, :] for a in range(PASSES)], [w2_sd] * PASSES, 4, t, h0, range(PASSES))
+                angle = ring.tile([P, BANK], F32, name="angle")
+                nc.scalar.activation(angle[:], acc_b[:], ACT.Abs, bias=ph_t[:, t : t + 1])
+                nc.scalar.activation(cosb[t][:, h0 : h0 + BANK], angle[:], ACT.Sin, bias=math.pi / 2, scale=-1.0)
+
+        flashes = {}
+
+        def flash(t, passes):
+            if t not in flashes:
+                flashes[t] = [psum.tile([P, BANK], F32, name=f"bank{FLASH_BANKS[t] + i}") for i in range(S // BANK)]
+            for acc_a, h0 in zip(flashes[t], range(0, S, BANK)):
+                first_stage(acc_a, w1_w, w1_s, 0, t, h0, passes)
+
+        phase(0)
+        for a in range(PASSES):
+            flash(0, [a])
+            flash(1, [a])
+        for t in range(1, PACK - 1):
+            phase(t)
 
         chunks = [slice(c0, c0 + CHUNK) for c0 in range(0, T2, CHUNK)]
         pairs = [keep.tile([P, 2, CHUNK, 2], BF16, name=f"pairs{c}") for c in range(len(chunks))]
         x_g = keep.tile([P, NX, PACK], BF16, name="x_g", align_bytes=64)
         for t in range(PACK):
-            feat = keep.tile([P, S], F32, name=f"feat{t}")
-            for h0 in range(0, S, BANK):
-                acc_a = psum_a.tile([P, BANK], F32, name="acc_a")
-                for a in range(PASSES):
-                    nc.tensor.matmul_mx(
-                        out=acc_a[:],
-                        lhsT=w1_w[a][:, t * P : (t + 1) * P].bitcast(FP8X4),
-                        lhsT_scale=w1_s[a][:, t * P : (t + 1) * P],
-                        rhs=v_w[a][:, h0 : h0 + BANK].bitcast(FP8X4),
-                        rhs_scale=v_s[4 * a : P, h0 : h0 + BANK],
-                        start=(a == 0),
-                        stop=(a == PASSES - 1),
-                    )
+            feat = ring.tile([P, S], F32, name="feat")
+            if 1 <= t < PACK - 1:
+                flash(t + 1, range(PASSES))
+            for acc_a, h0 in zip(flashes[t], range(0, S, BANK)):
                 nc.vector.scalar_tensor_tensor(
                     out=feat[:, h0 : h0 + BANK], in0=acc_a[:], scalar=gain_t[:, t : t + 1],
                     in1=cosb[t][:, h0 : h0 + BANK], op0=ALU.mult, op1=ALU.mult,
                 )
-            weights = wgs_first[:] if t == 0 else wgs_rest[:, t - 1, :]
-            nc.vector.tensor_tensor(page[t][:].indirect(idx2[:]), feat[:], weights, ALU.mult)
-            nc.sync.dma_start(out=out_1.rearrange("(p t) m -> t p m", t=PACK)[t], in_=page[t][:])
-            picked = ring.tile([P, NX], F32, name="picked")
+            if t == 0:
+                phase(PACK - 1)
+            nc.vector.tensor_tensor(page[t][:].indirect(idx2[:]), feat[:], wgs_t[t][:], ALU.mult)
+            queue = nc.scalar if t < PACK - 1 else nc.sync
+            queue.dma_start(out=out_1.rearrange("(p t) m -> t p m", t=PACK)[t], in_=page[t][:])
+            picked = keep.tile([P, NX], F32, name=f"picked{t}")
             nc.vector.tensor_copy(picked[:], page[t][:].indirect(idx3[:]))
             if t < PACK - 1:
                 nc.scalar.activation(x_g[:, :, t], picked[:], ACT.Copy, scale=cell_t[:, t : t + 1])
@@ -212,25 +234,19 @@ def tile_list_firefly_phase_board_kernel(
             nc.sync.dma_start(out=out_words[:, cols], in_=plane_w[:, cols])
 
         round_last(0)
-        round_last(1)
         nc.scalar.activation(x_g[:, :, t], picked[:], ACT.Copy, scale=cell_t[:, t : t + 1])
+        round_last(1)
         round_last(2)
         round_last(3)
         weave(0, nc.vector.tensor_copy, I32)
-        weave(1, nc.vector.tensor_copy, I32)
         quantise_page(0)
-        quantise_page(1)
         nc.vector.quantize_mx(out=x_w[:].bitcast(FP8X4), scales=x_s[:], in_=x_g[:].rearrange("p j t -> p (j t)"))
-        weave(2, nc.vector.tensor_copy, I32)
+        weave(1, nc.vector.tensor_copy, I32)
+        quantise_page(1)
+        weave(2, nc.scalar.copy, F32)
         weave(3, nc.scalar.copy, F32)
-        quantise_page(2)
-        quantise_page(3)
-        for q in range(QUADS):
-            nc.scalar.dma_start(
-                out=out_3[0, 4 * q : 4 * q + 4, :].bitcast(I32), in_=plane_s[32 * q : 32 * q + 4, :].bitcast(I32)
-            )
         for c in range(N // P):
-            acc_y = psum_b.tile([P, BANK], F32, name="acc_b")
+            acc_y = psum.tile([P, BANK], F32, name=f"bank{c}")
             nc.tensor.matmul_mx(
                 out=acc_y[:],
                 lhsT=w4_w[:, 2 * c * P : 2 * (c + 1) * P].bitcast(FP4X4),
@@ -243,3 +259,10 @@ def tile_list_firefly_phase_board_kernel(
             score = keep.tile([P, NX], F32, name=f"score{c}")
             nc.vector.tensor_tensor(score[:], acc_y[:], moon_t[:, c, :], ALU.min)
             nc.sync.dma_start(out=out_0[c * P : (c + 1) * P, :], in_=score[:])
+        quantise_page(2)
+        quantise_page(3)
+        for q in range(QUADS):
+            queue = nc.scalar if q % 2 else nc.sync
+            queue.dma_start(
+                out=out_3[0, 4 * q : 4 * q + 4, :].bitcast(I32), in_=plane_s[32 * q : 32 * q + 4, :].bitcast(I32)
+            )

@@ -133,7 +133,7 @@ def tile_list_firefly_phase_board_kernel(
                 v_w[1][:, h0 : h0 + BANK], tab_w[1][:].bitcast(U32).indirect(idx[:, h0 // 16 : (h0 + BANK) // 16])
             )
 
-        w1_g = [keep.tile([P, H * PACK], BF16, name=f"w1_g{a}", align_bytes=64) for a in range(PASSES)]
+        w1_g = [keep.tile([P, H * PACK], BF16, name=f"w1_g{a}", tag=f"tab_w{1 - a}", align_bytes=64) for a in range(PASSES)]
         w1_w = [keep.tile([P, H], U32, name=f"w1_w{a}", align_bytes=64) for a in range(PASSES)]
         w1_s = [keep.tile([P, H], U8, name=f"w1_s{a}", align_bytes=64) for a in range(PASSES)]
         for raw, (a, c0, c1) in zip(w1_raw, w1_parts):
@@ -182,25 +182,36 @@ def tile_list_firefly_phase_board_kernel(
         phase(0)
         for a in range(PASSES):
             flash(0, [a])
-            flash(1, [a])
+        flash(1, range(PASSES))
         for t in range(1, PACK - 1):
             phase(t)
 
         chunks = [slice(c0, c0 + CHUNK) for c0 in range(0, T2, CHUNK)]
         pairs = [keep.tile([P, 2, CHUNK, 2], BF16, name=f"pairs{c}") for c in range(len(chunks))]
         x_g = keep.tile([P, NX, PACK], BF16, name="x_g", align_bytes=64)
-        for t in range(PACK):
-            feat = ring.tile([P, S], F32, name="feat")
-            if 1 <= t < PACK - 1:
-                flash(t + 1, range(PASSES))
+        feats = [keep.tile([P, S], F32, name=f"feat{t}") for t in range(PACK)]
+        nc.vector.tensor_tensor(cosb[0][:], cosb[0][:], wgs_t[0][:], ALU.mult)
+        for acc_a, h0 in zip(flashes[0], range(0, S, BANK)):
+            nc.vector.scalar_tensor_tensor(
+                out=feats[0][:, h0 : h0 + BANK], in0=acc_a[:], scalar=gain_t[:, 0:1],
+                in1=cosb[0][:, h0 : h0 + BANK], op0=ALU.mult, op1=ALU.mult,
+            )
+
+        def features(t):
             for acc_a, h0 in zip(flashes[t], range(0, S, BANK)):
-                nc.vector.scalar_tensor_tensor(
-                    out=feat[:, h0 : h0 + BANK], in0=acc_a[:], scalar=gain_t[:, t : t + 1],
-                    in1=cosb[t][:, h0 : h0 + BANK], op0=ALU.mult, op1=ALU.mult,
-                )
-            if t == 0:
-                phase(PACK - 1)
-            nc.vector.tensor_tensor(page[t][:].indirect(idx2[:]), feat[:], wgs_t[t][:], ALU.mult)
+                nc.scalar.activation(feats[t][:, h0 : h0 + BANK], acc_a[:], ACT.Copy, scale=gain_t[:, t : t + 1])
+            nc.gpsimd.tensor_tensor(cosb[t][:], cosb[t][:], wgs_t[t][:], ALU.mult)
+            nc.gpsimd.tensor_tensor(feats[t][:], feats[t][:], cosb[t][:], ALU.mult)
+
+        features(1)
+        flash(2, range(PASSES))
+        features(2)
+        phase(3)
+        flash(3, range(PASSES))
+        features(3)
+        for t in range(PACK):
+            feat = feats[t]
+            nc.vector.tensor_copy(page[t][:].indirect(idx2[:]), feat[:])
             queue = nc.scalar if t < PACK - 1 else nc.sync
             queue.dma_start(out=out_1.rearrange("(p t) m -> t p m", t=PACK)[t], in_=page[t][:])
             picked = keep.tile([P, NX], F32, name=f"picked{t}")
@@ -234,15 +245,15 @@ def tile_list_firefly_phase_board_kernel(
             nc.sync.dma_start(out=out_words[:, cols], in_=plane_w[:, cols])
 
         round_last(0)
-        nc.scalar.activation(x_g[:, :, t], picked[:], ACT.Copy, scale=cell_t[:, t : t + 1])
         round_last(1)
+        nc.scalar.activation(x_g[:, :, t], picked[:], ACT.Copy, scale=cell_t[:, t : t + 1])
         round_last(2)
         round_last(3)
         weave(0, nc.vector.tensor_copy, I32)
-        quantise_page(0)
-        nc.vector.quantize_mx(out=x_w[:].bitcast(FP8X4), scales=x_s[:], in_=x_g[:].rearrange("p j t -> p (j t)"))
         weave(1, nc.vector.tensor_copy, I32)
+        quantise_page(0)
         quantise_page(1)
+        nc.vector.quantize_mx(out=x_w[:].bitcast(FP8X4), scales=x_s[:], in_=x_g[:].rearrange("p j t -> p (j t)"))
         weave(2, nc.scalar.copy, F32)
         weave(3, nc.scalar.copy, F32)
         for c in range(N // P):
@@ -262,7 +273,7 @@ def tile_list_firefly_phase_board_kernel(
         quantise_page(2)
         quantise_page(3)
         for q in range(QUADS):
-            queue = nc.scalar if q % 2 else nc.sync
+            queue = nc.sync if q < 2 else nc.scalar
             queue.dma_start(
                 out=out_3[0, 4 * q : 4 * q + 4, :].bitcast(I32), in_=plane_s[32 * q : 32 * q + 4, :].bitcast(I32)
             )

import math
from contextlib import ExitStack

import concourse.mybir as mybir

K, T, S, H, T2, NX, N = 1024, 4096, 1024, 512, 2048, 512, 384
FLOPS = 2 * K * H * S * 2 + 2 * H * N * NX

F32 = mybir.dt.float32
BF16 = mybir.dt.bfloat16
I32 = mybir.dt.int32
U32 = mybir.dt.uint32
U16 = mybir.dt.uint16
U8 = mybir.dt.uint8
FP8X4 = mybir.dt.float8_e4m3fn_x4
FP4X4 = mybir.dt.float4_e2m1fn_x4
ACT = mybir.ActivationFunctionType
ALU = mybir.AluOpType

P = 128
PACK = 4
PASSES = K // (P * PACK)
BANK = 512
QUADS = 4
QUAD_ORDER = (0, 2, 1, 3)
CHUNK = 512
PHASE_BANKS = (0, 2, 0, 4)
FLASH_BANKS = (4, 6, 2, 6)


def tile_list_firefly_phase_board_kernel(
    tc, tab_words, tab_scales, offs, offs2, offs3, w1, w2_words, w2_scales, ph, gain, wgs, page0, cell,
    w4_words, w4_scales, moon, out_0, out_1, out_2, out_3,
):
    nc = tc.nc
    with ExitStack() as ctx:
        keep = ctx.enter_context(tc.tile_pool(name="keep", bufs=1))
        ring = ctx.enter_context(tc.tile_pool(name="ring", bufs=2))
        psum = ctx.enter_context(tc.psum_pool(name="psum", bufs=1))

        idx = keep.tile([P, S // 16], U16, name="idx")
        idx2 = keep.tile([P, S // 16], U16, name="idx2")
        idx3 = keep.tile([P, NX // 16], U16, name="idx3")
        tab_w = [keep.tile([P, T], I32, name=f"tab_w{a}", align_bytes=64) for a in range(PASSES)]
        tab_s = keep.tile([P, T], U8, name="tab_s", align_bytes=64)
        v_s = keep.tile([P, PASSES * S], U8, name="v_s", align_bytes=64)
        w2_w = keep.tile([P, PASSES, H], I32, name="w2_w", align_bytes=64)
        w2_s = keep.tile([P, H], U8, name="w2_s", align_bytes=64)
        w4_w = keep.tile([P, 2 * N], U8, name="w4_w", align_bytes=64)
        w4_s = keep.tile([P, N], U8, name="w4_s", align_bytes=64)
        ph_t = keep.tile([P, PACK], F32, name="ph_t")
        gain_t = keep.tile([P, PACK], F32, name="gain_t")
        cell_t = keep.tile([P, PACK], F32, name="cell_t")
        w1_parts = [(0, 0, H), (1, 0, H // 2), (1, H // 2, H)]
        w1_raw = [keep.tile([P, PACK, c1 - c0], F32, name=f"w1_raw{i}") for i, (a, c0, c1) in enumerate(w1_parts)]
        wgs_t = [keep.tile([P, S], F32, name=f"wgs{t}") for t in range(PACK)]
        page = [keep.tile([P, T2], F32, name=f"page{t}") for t in range(PACK)]
        moon_t = keep.tile([P, N // P, NX], F32, name="moon_t")

        warm = keep.tile([P, 2], F32, name="warm")
        nc.vector.memset(warm[:, 0:1], 0.0)
        nc.scalar.activation(warm[:, 1:2], warm[:, 0:1], ACT.Sin)

        for plane in (tab_s, w2_s, v_s, w4_s):
            nc.vector.memset(plane[:].bitcast(I32), 0)

        def load_table(a):
            nc.sync.dma_start(out=tab_w[a][:], in_=tab_words[a].rearrange("p t i -> p (t i)").bitcast(I32))

        def load_page(t):
            nc.sync.dma_start(out=page[t][:], in_=page0.rearrange("(p t) m -> t p m", t=PACK)[t])

        def load_wgs(t):
            for q in QUAD_ORDER:
                nc.sync.dma_start(
                    out=wgs_t[t][32 * q : 32 * q + 32, :], in_=wgs.rearrange("(p t) j -> p t j", t=PACK)[:, t, :]
                )

        nc.sync.dma_start(out=w2_w[:], in_=w2_words.rearrange("a p c i -> p a (c i)").bitcast(I32))
        nc.sync.dma_start(idx[:], offs)
        for a in range(PASSES):
            nc.sync.dma_start(out=tab_s[4 * a : P : 8, :].bitcast(I32), in_=tab_scales[a].bitcast(I32))
        nc.sync.dma_start(out=ph_t[:], in_=ph.rearrange("(p t) -> p t", t=PACK))
        nc.sync.dma_start(out=gain_t[:], in_=gain.rearrange("(p t) -> p t", t=PACK))
        nc.sync.dma_start(idx2[:], offs2)
        load_table(0)
        for q in range(QUADS):
            nc.sync.dma_start(
                out=w2_s[32 * q : 32 * q + 4 * PASSES, :].bitcast(I32),
                in_=w2_scales[:, 4 * q : 4 * q + 4, :].bitcast(I32),
            )
        load_table(1)
        v_rows = keep.tile([P, S], U8, name="v_rows", align_bytes=64)
        nc.vector.tensor_copy(v_rows[:], tab_s[:].indirect(idx[:]))
        for q in range(QUADS):
            nc.sync.dma_start(
                out=v_s[32 * q : 32 * q + 4, :].bitcast(I32), in_=v_rows[32 * q : 32 * q + 32 : 4, :].bitcast(I32)
            )
        for raw, (a, c0, c1) in zip(w1_raw, w1_parts):
            rows = w1[a * P * PACK : (a + 1) * P * PACK, c0:c1]
            nc.sync.dma_start(out=raw[:], in_=rows.rearrange("(p j) c -> p j c", j=PACK))
        load_wgs(0)
        load_page(0)
        nc.sync.dma_start(idx3[:], offs3)
        nc.sync.dma_start(out=cell_t[:], in_=cell.rearrange("(p t) -> p t", t=PACK))
        for t in range(1, PACK):
            load_wgs(t)
            load_page(t)
        nc.sync.dma_start(out=w4_w[:].bitcast(I32), in_=w4_words[0].bitcast(I32))
        for q in range(QUADS):
            nc.sync.dma_start(
                out=w4_s[32 * q : 32 * q + 4, :].bitcast(I32),
                in_=w4_scales[0, 4 * q : 4 * q + 4, :].bitcast(I32),
            )
        nc.sync.dma_start(out=moon_t[:], in_=moon.rearrange("(c p) j -> p c j", p=P))

        v_w = [keep.tile([P, S], U32, name=f"v_w{a}", align_bytes=64) for a in range(PASSES)]
        nc.vector.tensor_copy(v_w[0][:], tab_w[0][:].bitcast(U32).indirect(idx[:]))

        w2_wd = keep.tile([P, PASSES, H], I32, name="w2_wd", align_bytes=64)
        w2_sd = keep.tile([P, H], U8, name="w2_sd", align_bytes=64)
        nc.vector.tensor_copy(
            out=w2_sd[:].rearrange("p (t m) -> p m t", t=PACK), in_=w2_s[:].rearrange("p (m t) -> p m t", t=PACK)
        )
        for a in range(PASSES):
            nc.vector.tensor_copy(
                out=w2_wd[:, a, :].rearrange("p (t c i) -> p c t i", t=PACK, i=4),
                in_=w2_w[:, a, :].rearrange("p (c i t) -> p c t i", t=PACK, i=4),
            )

        for h0 in range(0, S, BANK):
            nc.vector.tensor_copy(
                v_w[1][:, h0 : h0 + BANK], tab_w[1][:].bitcast(U32).indirect(idx[:, h0 // 16 : (h0 + BANK) // 16])
            )

        w1_g = [keep.tile([P, H * PACK], BF16, name=f"w1_g{a}", tag=f"tab_w{1 - a}", align_bytes=64) for a in range(PASSES)]
        w1_w = [keep.tile([P, H], U32, name=f"w1_w{a}", align_bytes=64) for a in range(PASSES)]
        w1_s = [keep.tile([P, H], U8, name=f"w1_s{a}", align_bytes=64) for a in range(PASSES)]
        for raw, (a, c0, c1) in zip(w1_raw, w1_parts):
            nc.vector.tensor_copy(
                out=w1_g[a][:].rearrange("p (t m j) -> p m t j", t=PACK, j=PACK)[:, c0 // PACK : c1 // PACK],
                in_=raw[:].rearrange("p j (m t) -> p m t j", t=PACK),
            )
            if c1 == H:
                for n0, n1 in ((0, H),) if a == 0 else ((0, P), (P, 2 * P), (2 * P, H)):
                    nc.vector.quantize_mx(
                        out=w1_w[a][:, n0:n1].bitcast(FP8X4),
                        scales=w1_s[a][:, n0:n1],
                        in_=w1_g[a][:, PACK * n0 : PACK * n1],
                    )

        def first_stage(acc, words, scales, first_row, t, h0, passes):
            for a in passes:
                nc.tensor.matmul_mx(
                    out=acc[:],
                    lhsT=words[a][:, t * P : (t + 1) * P].bitcast(FP8X4),
                    lhsT_scale=scales[a][first_row * a : P, t * P : (t + 1) * P],
                    rhs=v_w[a][:, h0 : h0 + BANK].bitcast(FP8X4),
                    rhs_scale=v_s[:, a * S + h0 : a * S + h0 + BANK],
                    start=(a == 0),
                    stop=(a == PASSES - 1),
                )

        cosb = [keep.tile([P, S], F32, name=f"cosb{t}") for t in range(PACK)]

        def phase(t):
            for h0 in range(0, S, BANK):
                acc_b = psum.tile([P, BANK], F32, name=f"bank{PHASE_BANKS[t] + h0 // BANK}")
                first_stage(acc_b, [w2_wd[:, a, :] for a in range(PASSES)], [w2_sd] * PASSES, 4, t, h0, range(PASSES))
                angle = ring.tile([P, BANK], F32, name="angle")
                nc.scalar.activation(angle[:], acc_b[:], ACT.Abs, bias=ph_t[:, t : t + 1])
                nc.scalar.activation(cosb[t][:, h0 : h0 + BANK], angle[:], ACT.Sin, bias=math.pi / 2, scale=-1.0)

        flashes = {}

        def flash(t, passes):
            if t not in flashes:
                flashes[t] = [psum.tile([P, BANK], F32, name=f"bank{FLASH_BANKS[t] + i}") for i in range(S // BANK)]
            for acc_a, h0 in zip(flashes[t], range(0, S, BANK)):
                first_stage(acc_a, w1_w, w1_s, 0, t, h0, passes)

        phase(0)
        for a in range(PASSES):
            flash(0, [a])
        flash(1, range(PASSES))
        for t in range(1, PACK - 1):
            phase(t)

        chunks = [slice(c0, c0 + CHUNK) for c0 in range(0, T2, CHUNK)]
        pairs = [keep.tile([P, 2, CHUNK, 2], BF16, name=f"pairs{c}") for c in range(len(chunks))]
        x_g = keep.tile([P, NX, PACK], BF16, name="x_g", align_bytes=64)
        feats = [keep.tile([P, S], F32, name=f"feat{t}") for t in range(PACK)]
        nc.vector.tensor_tensor(cosb[0][:], cosb[0][:], wgs_t[0][:], ALU.mult)
        for acc_a, h0 in zip(flashes[0], range(0, S, BANK)):
            nc.vector.scalar_tensor_tensor(
                out=feats[0][:, h0 : h0 + BANK], in0=acc_a[:], scalar=gain_t[:, 0:1],
                in1=cosb[0][:, h0 : h0 + BANK], op0=ALU.mult, op1=ALU.mult,
            )

        def features(t):
            for acc_a, h0 in zip(flashes[t], range(0, S, BANK)):
                nc.scalar.activation(feats[t][:, h0 : h0 + BANK], acc_a[:], ACT.Copy, scale=gain_t[:, t : t + 1])
            nc.gpsimd.tensor_tensor(cosb[t][:], cosb[t][:], wgs_t[t][:], ALU.mult)
            nc.gpsimd.tensor_tensor(feats[t][:], feats[t][:], cosb[t][:], ALU.mult)

        features(1)
        flash(2, range(PASSES))
        features(2)
        phase(3)
        flash(3, range(PASSES))
        features(3)
        for t in range(PACK):
            feat = feats[t]
            nc.vector.tensor_copy(page[t][:].indirect(idx2[:]), feat[:])
            queue = nc.scalar if t < PACK - 1 else nc.sync
            queue.dma_start(out=out_1.rearrange("(p t) m -> t p m", t=PACK)[t], in_=page[t][:])
            picked = keep.tile([P, NX], F32, name=f"picked{t}")
            nc.vector.tensor_copy(picked[:], page[t][:].indirect(idx3[:]))
            if t < PACK - 1:
                nc.scalar.activation(x_g[:, :, t], picked[:], ACT.Copy, scale=cell_t[:, t : t + 1])
                for c, cols in enumerate(chunks):
                    nc.scalar.copy(pairs[c][:, t // 2, :, t % 2], page[t][:, cols])

        t = PACK - 1
        plane_w = keep.tile([P, T2], I32, name="plane_w", align_bytes=64)
        plane_s = keep.tile([P, T2], U8, name="plane_s", align_bytes=64)
        x_w = keep.tile([P, NX], U32, name="x_w", align_bytes=64)
        x_s = keep.tile([P, NX], U8, name="x_s", align_bytes=64)
        out_words = out_2[0].rearrange("p m t -> p (m t)").bitcast(I32)

        grouped = [keep.tile([P, CHUNK * PACK], BF16, name=f"grouped{c}", align_bytes=64) for c in range(len(chunks))]

        def round_last(c):
            nc.scalar.copy(pairs[c][:, t // 2, :, t % 2], page[t][:, chunks[c]])

        def weave(c, copy, word):
            copy(
                grouped[c][:].bitcast(word).rearrange("p (m u) -> p m u", u=2),
                pairs[c][:].rearrange("p u m e -> p u (m e)").bitcast(word).rearrange("p u m -> p m u"),
            )

        def quantise_page(c):
            cols = chunks[c]
            nc.vector.quantize_mx(out=plane_w[:, cols].bitcast(FP8X4), scales=plane_s[:, cols], in_=grouped[c][:])
            nc.sync.dma_start(out=out_words[:, cols], in_=plane_w[:, cols])

        round_last(0)
        round_last(1)
        nc.scalar.activation(x_g[:, :, t], picked[:], ACT.Copy, scale=cell_t[:, t : t + 1])
        round_last(2)
        round_last(3)
        weave(0, nc.vector.tensor_copy, I32)
        weave(1, nc.vector.tensor_copy, I32)
        quantise_page(0)
        quantise_page(1)
        nc.vector.quantize_mx(out=x_w[:].bitcast(FP8X4), scales=x_s[:], in_=x_g[:].rearrange("p j t -> p (j t)"))
        weave(2, nc.scalar.copy, F32)
        weave(3, nc.scalar.copy, F32)
        for c in range(N // P):
            acc_y = psum.tile([P, BANK], F32, name=f"bank{c}")
            nc.tensor.matmul_mx(
                out=acc_y[:],
                lhsT=w4_w[:, 2 * c * P : 2 * (c + 1) * P].bitcast(FP4X4),
                lhsT_scale=w4_s[:, c * P : (c + 1) * P],
                rhs=x_w[:].bitcast(FP8X4),
                rhs_scale=x_s[:],
                start=True,
                stop=True,
            )
            score = keep.tile([P, NX], F32, name=f"score{c}")
            nc.vector.tensor_tensor(score[:], acc_y[:], moon_t[:, c, :], ALU.min)
            nc.sync.dma_start(out=out_0[c * P : (c + 1) * P, :], in_=score[:])
        quantise_page(2)
        quantise_page(3)
        for q in range(QUADS):
            queue = nc.sync if q < 2 else nc.scalar
            queue.dma_start(
                out=out_3[0, 4 * q : 4 * q + 4, :].bitcast(I32), in_=plane_s[32 * q : 32 * q + 4, :].bitcast(I32)
            )
